import numpy as np, ml_dtypes
CORES = [12,28,44,60,3,19,35,51]
N = 8
F = 32
def setup_inputs(rng):
    x = (rng.standard_normal((N, 128, 128), dtype=np.float32) / 11).astype(ml_dtypes.bfloat16)
    w = rng.standard_normal((128, F), dtype=np.float32).astype(ml_dtypes.bfloat16)
    return {"x": x, "xt": x.transpose(0, 2, 1).copy(), "w": np.broadcast_to(w, (N, 128, F)).copy()}
def setup_inputs_big(rng):
    d = setup_inputs(rng)
    for k in ("x", "xt", "w"): d[k] = (d[k].astype(np.float32) * 1024.0).astype(d[k].dtype)
    return d
def setup_inputs_small(rng):
    d = setup_inputs(rng)
    for k in ("x", "xt", "w"): d[k] = (d[k].astype(np.float32) * (1 / 1024.0)).astype(d[k].dtype)
    return d
def setup_inputs_apart(rng):
    d = setup_inputs(rng)
    f = (10.0 ** rng.permutation(np.linspace(-1.5, 1.5, N))).astype(np.float32).reshape(N, 1, 1)
    for k in ("x", "xt"): d[k] = (d[k].astype(np.float32) * f).astype(d[k].dtype)
    return d
def tie_inputs(x):
    x = dict(x)
    x["xt"] = x["x"].transpose(0, 2, 1).copy(); x["w"] = np.broadcast_to(x["w"][0], x["w"].shape).copy()
    return x
def reference(x, xt, w):
    X, XT, W = x.astype(np.float64), xt.astype(np.float64), w.astype(np.float64)
    s = sum(X[j].T @ (XT[j].T @ W[j]) for j in range(N)).astype(ml_dtypes.bfloat16 if x.dtype != np.float64 else np.float64)
    return {"y": np.broadcast_to(s, (N,) + s.shape)}

@@ -1,0 +1,102 @@
+from concourse.bass import DstId, RemoteDMATransfer
+
+N = 8
+F = 32
+K1 = 8
+
+SCRATCH = {
+    "xs": ("sbuf", [128, 128], "bfloat16"),
+    "ws": ("sbuf", [128, F], "bfloat16"),
+    "gs": ("sbuf", [128, 128], "bfloat16"),
+    "ps": ("sbuf", [128, F], "bfloat16"),
+    "gp": ("psum", [128, 512], "float32"),
+    "pp": ("psum", [128, 512], "float32"),
+    "gath": ("dram", [N, 128, F], "bfloat16"),
+    "res": ("dram", [128, F], "bfloat16"),
+}
+SEMAPHORES = ["ldx", "ldw", "mm1", "cp1", "mm2", "cp2", "arr", "sent", "done", "st"]
+
+
+def _bits(mask):
+    return [b for b in range(mask.bit_length()) if (mask >> b) & 1]
+
+
+def _low(mask, k):
+    m = 0
+    for b in _bits(mask)[:k]:
+        m |= 1 << b
+    return m
+
+
+def _links(topo, a, b):
+    ca, cb = topo.chip(a), topo.chip(b)
+    if ca == cb:
+        return 0
+    return 1 if (topo.mates(ca, cb) or topo.same_plane(ca, cb)) else 2
+
+
+def _hub(T, topo):
+    best = None
+    for h in range(max(T.cores) + 1):
+        if h in T.cores:
+            continue
+        if not all(topo.may_write(r, h) and topo.may_write(h, r) for r in T.cores):
+            continue
+        far = [_links(topo, r, h) + (1 if topo.die(r) != topo.die(h) else 0) for r in T.cores]
+        key = (max(far), sum(far), h)
+        if best is None or key < best:
+            best = key
+    return best[2]
+
+
+def _k1(topo, r, hub):
+    return min(K1, len(_bits(topo.mask(r, hub))))
+
+
+def rank_program(g, core, T, topo):
+    S = T.sem
+    hub = _hub(T, topo)
+    rank = T.rank_of(core)
+
+    if core == hub:
+        g.wait_ge(S.arr, sum(_k1(topo, r, hub) for r in T.cores))
+        free = 0
+        for r in T.cores:
+            free |= topo.mask(hub, r)
+        trs = []
+        for r in sorted(T.cores, key=lambda c: len(_bits(topo.mask(hub, c)))):
+            m = _low(topo.mask(hub, r) & free, 1)
+            free &= ~m
+            rid, pid, _se = topo.addr(r)
+            trs.append(RemoteDMATransfer(dst_ids=[DstId(rid=rid, pnc=pid)], dma_engine_mask=m, remote_sem=S.done,
+                                         srcs=[T.gath[j] for j in range(N)], dsts=[T.res[:]], alu_op=1))
+        g.remote_dma_fused(trs, local_sem=S.sent)
+        g.wait_ge(S.sent, len(trs))
+        return
+
+    if rank is None:
+        return
+
+    g.sync.dma_start(T.xs[:], T.x[:]).then_inc(S.ldx, 16)
+    g.scalar.dma_start(T.ws[:], T.w[:]).then_inc(S.ldw, 16)
+
+    g.tensor.wait_ge(S.ldx, 16)
+    g.tensor.matmul(T.gp[:, 0:128], T.xs[:], T.xs[:], start=True, stop=True).then_inc(S.mm1, 1)
+    g.vector.wait_ge(S.mm1, 1)
+    g.vector.tensor_copy(T.gs[:], T.gp[:, 0:128]).then_inc(S.cp1, 1)
+    g.tensor.wait_ge(S.ldw, 16)
+    g.tensor.wait_ge(S.cp1, 1)
+    g.tensor.matmul(T.pp[:, 0:F], T.gs[:], T.ws[:], start=True, stop=True).then_inc(S.mm2, 1)
+    g.vector.wait_ge(S.mm2, 1)
+    g.vector.tensor_copy(T.ps[:], T.pp[:, 0:F]).then_inc(S.cp2, 1)
+
+    k = _k1(topo, core, hub)
+    rid, pid, _se = topo.addr(hub)
+    g.wait_ge(S.cp2, 1)
+    g.remote_dma(out_ap=T.gath[rank], in_ap=T.ps[:], remote_sem=S.arr, local_sem=S.sent, pid=pid, routing_id=rid,
+                 dma_engine_mask=_low(topo.mask(core, hub), k))
+
+    g.sync.wait_ge(S.done, 1)
+    g.sync.dma_start(T.y[:], T.res[:]).then_inc(S.st, 16)
+    g.sync.wait_ge(S.st, 16)
+    g.wait_ge(S.sent, k)

@@ -2,7 +2,10 @@ from concourse.bass import DstId, RemoteDMATransfer
 
 N = 8
 F = 32
+H = 2
 K1 = 8
+K2 = 8
+TPH = 2
 
 SCRATCH = {
     "xs": ("sbuf", [128, 128], "bfloat16"),
@@ -21,9 +24,14 @@ def _bits(mask):
     return [b for b in range(mask.bit_length()) if (mask >> b) & 1]
 
 
-def _low(mask, k):
+def _spread(mask, k):
+    bits = _bits(mask)
+    return bits[::max(1, len(bits) // k)][:k]
+
+
+def _mask_of(engines):
     m = 0
-    for b in _bits(mask)[:k]:
+    for b in engines:
         m |= 1 << b
     return m
 
@@ -35,43 +43,84 @@ def _links(topo, a, b):
     return 1 if (topo.mates(ca, cb) or topo.same_plane(ca, cb)) else 2
 
 
-def _hub(T, topo):
-    best = None
+def _dst(topo, c):
+    rid, pid, _se = topo.addr(c)
+    return DstId(rid=rid, pnc=pid)
+
+
+def _common(topo, src, cores):
+    m = topo.mask(src, cores[0])
+    for c in cores:
+        m &= topo.mask(src, c)
+    return m
+
+
+def _hubs(T, topo):
+    keys = []
     for h in range(max(T.cores) + 1):
         if h in T.cores:
             continue
         if not all(topo.may_write(r, h) and topo.may_write(h, r) for r in T.cores):
             continue
         far = [_links(topo, r, h) + (1 if topo.die(r) != topo.die(h) else 0) for r in T.cores]
-        key = (max(far), sum(far), h)
-        if best is None or key < best:
-            best = key
-    return best[2]
+        keys.append((max(far), sum(far), h))
+    hubs = []
+    for _a, _b, h in sorted(keys):
+        if len(hubs) < H and all(topo.chip(h) != topo.chip(o) for o in hubs):
+            hubs.append(h)
+    return hubs
 
 
-def _k1(topo, r, hub):
-    return min(K1, len(_bits(topo.mask(r, hub))))
+def _served(T, topo, hubs):
+    served = {h: [] for h in hubs}
+    ties = []
+    for r in T.cores:
+        d = [_links(topo, h, r) for h in hubs]
+        if d.count(min(d)) == 1:
+            served[hubs[d.index(min(d))]].append(r)
+        else:
+            ties.append(r)
+    for r in ties:
+        served[min(hubs, key=lambda h: len(served[h]))].append(r)
+    return served
+
+
+def _transfers(topo, hub, ranks):
+    ch = topo.chip(hub)
+    far_first = sorted(ranks, key=lambda r: -_links(topo, hub, r))
+    kinds = [[r for r in far_first if topo.chip(r) != ch and not topo.same_plane(ch, topo.chip(r))], []]
+    kinds[1] = [r for r in far_first if r not in kinds[0]]
+    out = [[] for _i in range(TPH)]
+    turn = 0
+    while kinds[0] or kinds[1]:
+        for i in range(TPH):
+            k = (i + turn) % 2
+            if not kinds[k]:
+                k = 1 - k
+            if kinds[k]:
+                out[i].append(kinds[k].pop(0))
+        turn += 1
+    return out
 
 
 def rank_program(g, core, T, topo):
     S = T.sem
-    hub = _hub(T, topo)
+    hubs = _hubs(T, topo)
     rank = T.rank_of(core)
+    per = K2 // TPH
 
-    if core == hub:
-        g.wait_ge(S.arr, sum(_k1(topo, r, hub) for r in T.cores))
-        free = 0
-        for r in T.cores:
-            free |= topo.mask(hub, r)
+    if core in hubs:
+        mine = _served(T, topo, hubs)[core]
+        g.wait_ge(S.arr, N * K1)
+        engines = _spread(_common(topo, core, mine), K2)
         trs = []
-        for r in sorted(T.cores, key=lambda c: len(_bits(topo.mask(hub, c)))):
-            m = _low(topo.mask(hub, r) & free, 1)
-            free &= ~m
-            rid, pid, _se = topo.addr(r)
-            trs.append(RemoteDMATransfer(dst_ids=[DstId(rid=rid, pnc=pid)], dma_engine_mask=m, remote_sem=S.done,
-                                         srcs=[T.gath[j] for j in range(N)], dsts=[T.res[:]], alu_op=1))
+        for i, grp in enumerate(_transfers(topo, core, mine)):
+            trs.append(RemoteDMATransfer(dst_ids=[_dst(topo, r) for r in grp],
+                                         dma_engine_mask=_mask_of(engines[i * per:(i + 1) * per]),
+                                         remote_sem=S.done, srcs=[T.gath[j] for j in range(N)],
+                                         dsts=[T.res[:] for r in grp], alu_op=1))
         g.remote_dma_fused(trs, local_sem=S.sent)
-        g.wait_ge(S.sent, len(trs))
+        g.wait_ge(S.sent, per * len(trs))
         return
 
     if rank is None:
@@ -90,13 +139,13 @@ def rank_program(g, core, T, topo):
     g.vector.wait_ge(S.mm2, 1)
     g.vector.tensor_copy(T.ps[:], T.pp[:, 0:F]).then_inc(S.cp2, 1)
 
-    k = _k1(topo, core, hub)
-    rid, pid, _se = topo.addr(hub)
     g.wait_ge(S.cp2, 1)
-    g.remote_dma(out_ap=T.gath[rank], in_ap=T.ps[:], remote_sem=S.arr, local_sem=S.sent, pid=pid, routing_id=rid,
-                 dma_engine_mask=_low(topo.mask(core, hub), k))
+    tr = RemoteDMATransfer(dst_ids=[_dst(topo, h) for h in hubs],
+                           dma_engine_mask=_mask_of(_spread(_common(topo, core, hubs), K1)),
+                           remote_sem=S.arr, srcs=[T.ps[:]], dsts=[T.gath[rank] for h in hubs], alu_op=0)
+    g.remote_dma_fused([tr], local_sem=S.sent)
 
-    g.sync.wait_ge(S.done, 1)
+    g.sync.wait_ge(S.done, per)
     g.sync.dma_start(T.y[:], T.res[:]).then_inc(S.st, 16)
     g.sync.wait_ge(S.st, 16)
-    g.wait_ge(S.sent, k)
+    g.wait_ge(S.sent, K1)

@@ -1,37 +1,35 @@
 from concourse.bass import DstId, RemoteDMATransfer
+from concourse.mybir import AluOpType
 
 N = 8
 F = 32
-H = 2
-K1 = 8
-K2 = 8
-TPH = 2
+NCORES = 64
+KH = 2
+KA = 8
+KD = 8
+KF = 8
 
 SCRATCH = {
     "xs": ("sbuf", [128, 128], "bfloat16"),
     "ws": ("sbuf", [128, F], "bfloat16"),
     "gs": ("sbuf", [128, 128], "bfloat16"),
     "ps": ("sbuf", [128, F], "bfloat16"),
+    "on": ("sbuf", [128, 128], "bfloat16"),
+    "idm": ("sbuf", [128, 128], "bfloat16"),
+    "ga": ("sbuf", [128, N * F], "bfloat16"),
+    "hb": ("sbuf", [128, F], "bfloat16"),
+    "ys": ("sbuf", [128, F], "bfloat16"),
     "gp": ("psum", [128, 512], "float32"),
     "pp": ("psum", [128, 512], "float32"),
-    "gath": ("dram", [N, 128, F], "bfloat16"),
-    "res": ("dram", [128, F], "bfloat16"),
+    "acc": ("psum", [128, 512], "float32"),
 }
-SEMAPHORES = ["ldx", "ldw", "mm1", "cp1", "mm2", "cp2", "arr", "sent", "done", "st"]
-
-
-def _bits(mask):
-    return [b for b in range(mask.bit_length()) if (mask >> b) & 1]
+SEMAPHORES = ["ldx", "ldw", "one", "idn", "mm1", "cp1", "mm2", "cp2", "harr", "a1", "a2", "sent", "mmf", "cpf", "st"]
 
 
 def _spread(mask, k):
-    bits = _bits(mask)
-    return bits[::max(1, len(bits) // k)][:k]
-
-
-def _mask_of(engines):
+    bits = [b for b in range(mask.bit_length()) if (mask >> b) & 1]
     m = 0
-    for b in engines:
+    for b in bits[::max(1, len(bits) // k)][:k]:
         m |= 1 << b
     return m
 
@@ -55,79 +53,57 @@ def _common(topo, src, cores):
     return m
 
 
-def _hubs(T, topo):
-    keys = []
-    for h in range(max(T.cores) + 1):
-        if h in T.cores:
-            continue
-        if not all(topo.may_write(r, h) and topo.may_write(h, r) for r in T.cores):
-            continue
-        far = [_links(topo, r, h) + (1 if topo.die(r) != topo.die(h) else 0) for r in T.cores]
-        keys.append((max(far), sum(far), h))
-    hubs = []
-    for _a, _b, h in sorted(keys):
-        if len(hubs) < H and all(topo.chip(h) != topo.chip(o) for o in hubs):
-            hubs.append(h)
-    return hubs
-
-
-def _served(T, topo, hubs):
-    served = {h: [] for h in hubs}
-    ties = []
+def _plan(T, topo):
+    plan = {}
     for r in T.cores:
-        d = [_links(topo, h, r) for h in hubs]
-        if d.count(min(d)) == 1:
-            served[hubs[d.index(min(d))]].append(r)
-        else:
-            ties.append(r)
-    for r in ties:
-        served[min(hubs, key=lambda h: len(served[h]))].append(r)
-    return served
+        others = [d for d in T.cores if d != r]
+        direct = [d for d in others if topo.may_write(r, d)]
+        rest = [d for d in others if not topo.may_write(r, d)]
+        fwd = {}
+        if rest:
+            cands = [h for h in range(NCORES)
+                     if topo.chip(h) == topo.chip(r) and h not in T.cores
+                     and all(topo.may_write(h, d) for d in rest)]
+            cands.sort(key=lambda h: (topo.die(h) != topo.die(r), h))
+            hs = cands[:KH]
+            rest = sorted(rest, key=lambda d: -_links(topo, r, d))
+            for i, h in enumerate(hs):
+                fwd[h] = rest[i::len(hs)]
+        plan[r] = (direct, fwd)
+    return plan
 
 
-def _transfers(topo, hub, ranks):
-    ch = topo.chip(hub)
-    far_first = sorted(ranks, key=lambda r: -_links(topo, hub, r))
-    kinds = [[r for r in far_first if topo.chip(r) != ch and not topo.same_plane(ch, topo.chip(r))], []]
-    kinds[1] = [r for r in far_first if r not in kinds[0]]
-    out = [[] for _i in range(TPH)]
-    turn = 0
-    while kinds[0] or kinds[1]:
-        for i in range(TPH):
-            k = (i + turn) % 2
-            if not kinds[k]:
-                k = 1 - k
-            if kinds[k]:
-                out[i].append(kinds[k].pop(0))
-        turn += 1
-    return out
+def _copy(topo, src_core, dests, k, sem, src, dst):
+    return RemoteDMATransfer(dst_ids=[_dst(topo, d) for d in dests],
+                             dma_engine_mask=_spread(_common(topo, src_core, dests), k),
+                             remote_sem=sem, srcs=[src], dsts=[dst for _d in dests], alu_op=0)
 
 
 def rank_program(g, core, T, topo):
     S = T.sem
-    hubs = _hubs(T, topo)
+    plan = _plan(T, topo)
     rank = T.rank_of(core)
-    per = K2 // TPH
-
-    if core in hubs:
-        mine = _served(T, topo, hubs)[core]
-        g.wait_ge(S.arr, N * K1)
-        engines = _spread(_common(topo, core, mine), K2)
-        trs = []
-        for i, grp in enumerate(_transfers(topo, core, mine)):
-            trs.append(RemoteDMATransfer(dst_ids=[_dst(topo, r) for r in grp],
-                                         dma_engine_mask=_mask_of(engines[i * per:(i + 1) * per]),
-                                         remote_sem=S.done, srcs=[T.gath[j] for j in range(N)],
-                                         dsts=[T.res[:] for r in grp], alu_op=1))
-        g.remote_dma_fused(trs, local_sem=S.sent)
-        g.wait_ge(S.sent, per * len(trs))
-        return
 
     if rank is None:
+        for r in T.cores:
+            if core in plan[r][1]:
+                j = T.rank_of(r)
+                g.wait_ge(S.harr, KA)
+                g.remote_dma_fused([_copy(topo, core, plan[r][1][core], KF, S.a2, T.hb[:],
+                                          T.ga[:, j * F:(j + 1) * F])], local_sem=S.sent)
+                g.wait_ge(S.sent, KF)
         return
+
+    direct, fwd = plan[core]
+    early = [T.rank_of(r) for r in T.cores if core in plan[r][0]]
+    late = [T.rank_of(r) for r in T.cores if any(core in ds for ds in plan[r][1].values())]
 
     g.sync.dma_start(T.xs[:], T.x[:]).then_inc(S.ldx, 16)
     g.scalar.dma_start(T.ws[:], T.w[:]).then_inc(S.ldw, 16)
+
+    g.vector.memset(T.on[:], 1.0).then_inc(S.one, 1)
+    g.wait_ge(S.one, 1)
+    g.affine_select(T.idm[:], T.on[:], [[-1, 128]], AluOpType.is_equal, 0.0, 0, 1).then_inc(S.idn, 1)
 
     g.tensor.wait_ge(S.ldx, 16)
     g.tensor.matmul(T.gp[:, 0:128], T.xs[:], T.xs[:], start=True, stop=True).then_inc(S.mm1, 1)
@@ -138,14 +114,31 @@ def rank_program(g, core, T, topo):
     g.tensor.matmul(T.pp[:, 0:F], T.gs[:], T.ws[:], start=True, stop=True).then_inc(S.mm2, 1)
     g.vector.wait_ge(S.mm2, 1)
     g.vector.tensor_copy(T.ps[:], T.pp[:, 0:F]).then_inc(S.cp2, 1)
+    g.tensor.matmul(T.acc[:, 0:F], T.gs[:], T.ws[:], start=True, stop=False)
 
+    slot = T.ga[:, rank * F:(rank + 1) * F]
     g.wait_ge(S.cp2, 1)
-    tr = RemoteDMATransfer(dst_ids=[_dst(topo, h) for h in hubs],
-                           dma_engine_mask=_mask_of(_spread(_common(topo, core, hubs), K1)),
-                           remote_sem=S.arr, srcs=[T.ps[:]], dsts=[T.gath[rank] for h in hubs], alu_op=0)
-    g.remote_dma_fused([tr], local_sem=S.sent)
+    sent = 0
+    if fwd:
+        g.remote_dma_fused([_copy(topo, core, sorted(fwd), KA, S.harr, T.ps[:], T.hb[:])], local_sem=S.sent)
+        sent += KA
+    g.remote_dma_fused([_copy(topo, core, direct, KD, S.a1, T.ps[:], slot)], local_sem=S.sent)
+    sent += KD
 
-    g.sync.wait_ge(S.done, per)
-    g.sync.dma_start(T.y[:], T.res[:]).then_inc(S.st, 16)
+    g.tensor.wait_ge(S.idn, 1)
+    g.tensor.wait_ge(S.a1, KD * len(early))
+    terms = early + late
+    for i, j in enumerate(terms):
+        if late and j == late[0]:
+            g.tensor.wait_ge(S.a2, KF * len(late))
+        mm = g.tensor.matmul(T.acc[:, 0:F], T.idm[:], T.ga[:, j * F:(j + 1) * F], start=False,
+                             stop=(i == len(terms) - 1))
+        if i == len(terms) - 1:
+            mm.then_inc(S.mmf, 1)
+    g.vector.wait_ge(S.mmf, 1)
+    g.vector.tensor_copy(T.ys[:], T.acc[:, 0:F]).then_inc(S.cpf, 1)
+
+    g.sync.wait_ge(S.cpf, 1)
+    g.sync.dma_start(T.y[:], T.ys[:]).then_inc(S.st, 16)
     g.sync.wait_ge(S.st, 16)
-    g.wait_ge(S.sent, K1)
+    g.wait_ge(S.sent, sent)

@@ -5,6 +5,7 @@ N = 8
 F = 32
 NCORES = 64
 KH = 2
+KR = 4
 KA = 8
 KD = 8
 KF = 8
@@ -14,16 +15,20 @@ SCRATCH = {
     "ws": ("sbuf", [128, F], "bfloat16"),
     "gs": ("sbuf", [128, 128], "bfloat16"),
     "ps": ("sbuf", [128, F], "bfloat16"),
+    "xn": ("sbuf", [128, 128], "bfloat16"),
+    "gn": ("sbuf", [128, 128], "bfloat16"),
     "on": ("sbuf", [128, 128], "bfloat16"),
     "idm": ("sbuf", [128, 128], "bfloat16"),
     "ga": ("sbuf", [128, N * F], "bfloat16"),
     "hb": ("sbuf", [128, F], "bfloat16"),
     "ys": ("sbuf", [128, F], "bfloat16"),
     "gp": ("psum", [128, 512], "float32"),
+    "gq": ("psum", [128, 512], "float32"),
     "pp": ("psum", [128, 512], "float32"),
     "acc": ("psum", [128, 512], "float32"),
 }
-SEMAPHORES = ["ldx", "ldw", "one", "idn", "mm1", "cp1", "mm2", "cp2", "harr", "a1", "a2", "sent", "mmf", "cpf", "st"]
+SEMAPHORES = ["ldx", "ldw", "one", "idn", "mm1", "cp1", "mm2", "cp2", "harr", "a1", "a2", "a3", "mm3", "cp3",
+              "sent", "mmf", "cpf", "st"]
 
 
 def _spread(mask, k):
@@ -69,13 +74,18 @@ def _plan(T, topo):
             rest = sorted(rest, key=lambda d: -_links(topo, r, d))
             for i, h in enumerate(hs):
                 fwd[h] = rest[i::len(hs)]
-        plan[r] = (direct, fwd)
+        plan[r] = [direct, fwd, None]
+    ring = [r for r in T.cores if plan[r][1]]
+    for i, r in enumerate(ring):
+        nb = ring[(i + 1) % len(ring)]
+        if nb in plan[r][0]:
+            plan[r][2] = nb
+            plan[r][0] = [d for d in plan[r][0] if d != nb]
     return plan
 
 
-def _copy(topo, src_core, dests, k, sem, src, dst):
-    return RemoteDMATransfer(dst_ids=[_dst(topo, d) for d in dests],
-                             dma_engine_mask=_spread(_common(topo, src_core, dests), k),
+def _copy(topo, dests, mask, sem, src, dst):
+    return RemoteDMATransfer(dst_ids=[_dst(topo, d) for d in dests], dma_engine_mask=mask,
                              remote_sem=sem, srcs=[src], dsts=[dst for _d in dests], alu_op=0)
 
 
@@ -88,15 +98,17 @@ def rank_program(g, core, T, topo):
         for r in T.cores:
             if core in plan[r][1]:
                 j = T.rank_of(r)
+                ds = plan[r][1][core]
                 g.wait_ge(S.harr, KA)
-                g.remote_dma_fused([_copy(topo, core, plan[r][1][core], KF, S.a2, T.hb[:],
+                g.remote_dma_fused([_copy(topo, ds, _spread(_common(topo, core, ds), KF), S.a2, T.hb[:],
                                           T.ga[:, j * F:(j + 1) * F])], local_sem=S.sent)
                 g.wait_ge(S.sent, KF)
         return
 
-    direct, fwd = plan[core]
+    direct, fwd, nb = plan[core]
     early = [T.rank_of(r) for r in T.cores if core in plan[r][0]]
     late = [T.rank_of(r) for r in T.cores if any(core in ds for ds in plan[r][1].values())]
+    raw = [r for r in T.cores if plan[r][2] == core]
 
     g.sync.dma_start(T.xs[:], T.x[:]).then_inc(S.ldx, 16)
     g.scalar.dma_start(T.ws[:], T.w[:]).then_inc(S.ldw, 16)
@@ -104,6 +116,13 @@ def rank_program(g, core, T, topo):
     g.vector.memset(T.on[:], 1.0).then_inc(S.one, 1)
     g.wait_ge(S.one, 1)
     g.affine_select(T.idm[:], T.on[:], [[-1, 128]], AluOpType.is_equal, 0.0, 0, 1).then_inc(S.idn, 1)
+
+    sent = 0
+    if nb is not None:
+        g.wait_ge(S.ldx, 16)
+        g.remote_dma_fused([_copy(topo, [nb], _spread(topo.mask(core, nb), KR), S.a3, T.xs[:], T.xn[:])],
+                           local_sem=S.sent)
+        sent += KR
 
     g.tensor.wait_ge(S.ldx, 16)
     g.tensor.matmul(T.gp[:, 0:128], T.xs[:], T.xs[:], start=True, stop=True).then_inc(S.mm1, 1)
@@ -118,22 +137,36 @@ def rank_program(g, core, T, topo):
 
     slot = T.ga[:, rank * F:(rank + 1) * F]
     g.wait_ge(S.cp2, 1)
-    sent = 0
     if fwd:
-        g.remote_dma_fused([_copy(topo, core, sorted(fwd), KA, S.harr, T.ps[:], T.hb[:])], local_sem=S.sent)
+        hs = sorted(fwd)
+        m = _common(topo, core, hs)
+        if nb is not None and _spread(m & ~topo.mask(core, nb), KA).bit_count() == KA:
+            m &= ~topo.mask(core, nb)
+        g.remote_dma_fused([_copy(topo, hs, _spread(m, KA), S.harr, T.ps[:], T.hb[:])], local_sem=S.sent)
         sent += KA
-    g.remote_dma_fused([_copy(topo, core, direct, KD, S.a1, T.ps[:], slot)], local_sem=S.sent)
+    g.remote_dma_fused([_copy(topo, direct, _spread(_common(topo, core, direct), KD), S.a1, T.ps[:], slot)],
+                       local_sem=S.sent)
     sent += KD
 
+    if raw:
+        g.tensor.wait_ge(S.a3, KR)
+        g.tensor.matmul(T.gq[:, 0:128], T.xn[:], T.xn[:], start=True, stop=True).then_inc(S.mm3, 1)
+        g.vector.wait_ge(S.mm3, 1)
+        g.vector.tensor_copy(T.gn[:], T.gq[:, 0:128]).then_inc(S.cp3, 1)
+
+    ops = [("p", j) for j in early] + [("g", 0) for _r in raw] + [("p", j) for j in late]
     g.tensor.wait_ge(S.idn, 1)
     g.tensor.wait_ge(S.a1, KD * len(early))
-    terms = early + late
-    for i, j in enumerate(terms):
-        if late and j == late[0]:
-            g.tensor.wait_ge(S.a2, KF * len(late))
-        mm = g.tensor.matmul(T.acc[:, 0:F], T.idm[:], T.ga[:, j * F:(j + 1) * F], start=False,
-                             stop=(i == len(terms) - 1))
-        if i == len(terms) - 1:
+    for i, (kind, j) in enumerate(ops):
+        last = i == len(ops) - 1
+        if kind == "g":
+            g.tensor.wait_ge(S.cp3, 1)
+            mm = g.tensor.matmul(T.acc[:, 0:F], T.gn[:], T.ws[:], start=False, stop=last)
+        else:
+            if late and j == late[0]:
+                g.tensor.wait_ge(S.a2, KF * len(late))
+            mm = g.tensor.matmul(T.acc[:, 0:F], T.idm[:], T.ga[:, j * F:(j + 1) * F], start=False, stop=last)
+        if last:
             mm.then_inc(S.mmf, 1)
     g.vector.wait_ge(S.mmf, 1)
     g.vector.tensor_copy(T.ys[:], T.acc[:, 0:F]).then_inc(S.cpf, 1)

from concourse.bass import DstId, RemoteDMATransfer
from concourse.mybir import AluOpType

N = 8
F = 32
NCORES = 64
KH = 2
KR = 4
KA = 8
KD = 8
KF = 8

SCRATCH = {
    "xs": ("sbuf", [128, 128], "bfloat16"),
    "ws": ("sbuf", [128, F], "bfloat16"),
    "gs": ("sbuf", [128, 128], "bfloat16"),
    "ps": ("sbuf", [128, F], "bfloat16"),
    "xn": ("sbuf", [128, 128], "bfloat16"),
    "gn": ("sbuf", [128, 128], "bfloat16"),
    "on": ("sbuf", [128, 128], "bfloat16"),
    "idm": ("sbuf", [128, 128], "bfloat16"),
    "ga": ("sbuf", [128, N * F], "bfloat16"),
    "hb": ("sbuf", [128, F], "bfloat16"),
    "ys": ("sbuf", [128, F], "bfloat16"),
    "gp": ("psum", [128, 512], "float32"),
    "gq": ("psum", [128, 512], "float32"),
    "pp": ("psum", [128, 512], "float32"),
    "acc": ("psum", [128, 512], "float32"),
}
SEMAPHORES = ["ldx", "ldw", "one", "idn", "mm1", "cp1", "mm2", "cp2", "harr", "a1", "a2", "a3", "mm3", "cp3",
              "sent", "mmf", "cpf", "st"]


def _spread(mask, k):
    bits = [b for b in range(mask.bit_length()) if (mask >> b) & 1]
    m = 0
    for b in bits[::max(1, len(bits) // k)][:k]:
        m |= 1 << b
    return m


def _links(topo, a, b):
    ca, cb = topo.chip(a), topo.chip(b)
    if ca == cb:
        return 0
    return 1 if (topo.mates(ca, cb) or topo.same_plane(ca, cb)) else 2


def _dst(topo, c):
    rid, pid, _se = topo.addr(c)
    return DstId(rid=rid, pnc=pid)


def _common(topo, src, cores):
    m = topo.mask(src, cores[0])
    for c in cores:
        m &= topo.mask(src, c)
    return m


def _plan(T, topo):
    plan = {}
    for r in T.cores:
        others = [d for d in T.cores if d != r]
        direct = [d for d in others if topo.may_write(r, d)]
        rest = [d for d in others if not topo.may_write(r, d)]
        fwd = {}
        if rest:
            cands = [h for h in range(NCORES)
                     if topo.chip(h) == topo.chip(r) and h not in T.cores
                     and all(topo.may_write(h, d) for d in rest)]
            cands.sort(key=lambda h: (topo.die(h) != topo.die(r), h))
            hs = cands[:KH]
            rest = sorted(rest, key=lambda d: -_links(topo, r, d))
            for i, h in enumerate(hs):
                fwd[h] = rest[i::len(hs)]
        plan[r] = [direct, fwd, None]
    ring = [r for r in T.cores if plan[r][1]]
    for i, r in enumerate(ring):
        nb = ring[(i + 1) % len(ring)]
        if nb in plan[r][0]:
            plan[r][2] = nb
            plan[r][0] = [d for d in plan[r][0] if d != nb]
    return plan


def _copy(topo, dests, mask, sem, src, dst):
    return RemoteDMATransfer(dst_ids=[_dst(topo, d) for d in dests], dma_engine_mask=mask,
                             remote_sem=sem, srcs=[src], dsts=[dst for _d in dests], alu_op=0)


def rank_program(g, core, T, topo):
    S = T.sem
    plan = _plan(T, topo)
    rank = T.rank_of(core)

    if rank is None:
        for r in T.cores:
            if core in plan[r][1]:
                j = T.rank_of(r)
                ds = plan[r][1][core]
                g.wait_ge(S.harr, KA)
                g.remote_dma_fused([_copy(topo, ds, _spread(_common(topo, core, ds), KF), S.a2, T.hb[:],
                                          T.ga[:, j * F:(j + 1) * F])], local_sem=S.sent)
                g.wait_ge(S.sent, KF)
        return

    direct, fwd, nb = plan[core]
    early = [T.rank_of(r) for r in T.cores if core in plan[r][0]]
    late = [T.rank_of(r) for r in T.cores if any(core in ds for ds in plan[r][1].values())]
    raw = [r for r in T.cores if plan[r][2] == core]

    g.sync.dma_start(T.xs[:], T.x[:]).then_inc(S.ldx, 16)
    g.scalar.dma_start(T.ws[:], T.w[:]).then_inc(S.ldw, 16)

    g.vector.memset(T.on[:], 1.0).then_inc(S.one, 1)
    g.wait_ge(S.one, 1)
    g.affine_select(T.idm[:], T.on[:], [[-1, 128]], AluOpType.is_equal, 0.0, 0, 1).then_inc(S.idn, 1)

    sent = 0
    if nb is not None:
        g.wait_ge(S.ldx, 16)
        g.remote_dma_fused([_copy(topo, [nb], _spread(topo.mask(core, nb), KR), S.a3, T.xs[:], T.xn[:])],
                           local_sem=S.sent)
        sent += KR

    g.tensor.wait_ge(S.ldx, 16)
    g.tensor.matmul(T.gp[:, 0:128], T.xs[:], T.xs[:], start=True, stop=True).then_inc(S.mm1, 1)
    g.vector.wait_ge(S.mm1, 1)
    g.vector.tensor_copy(T.gs[:], T.gp[:, 0:128]).then_inc(S.cp1, 1)
    g.tensor.wait_ge(S.ldw, 16)
    g.tensor.wait_ge(S.cp1, 1)
    g.tensor.matmul(T.pp[:, 0:F], T.gs[:], T.ws[:], start=True, stop=True).then_inc(S.mm2, 1)
    g.vector.wait_ge(S.mm2, 1)
    g.vector.tensor_copy(T.ps[:], T.pp[:, 0:F]).then_inc(S.cp2, 1)
    g.tensor.matmul(T.acc[:, 0:F], T.gs[:], T.ws[:], start=True, stop=False)

    slot = T.ga[:, rank * F:(rank + 1) * F]
    g.wait_ge(S.cp2, 1)
    if fwd:
        hs = sorted(fwd)
        m = _common(topo, core, hs)
        if nb is not None and _spread(m & ~topo.mask(core, nb), KA).bit_count() == KA:
            m &= ~topo.mask(core, nb)
        g.remote_dma_fused([_copy(topo, hs, _spread(m, KA), S.harr, T.ps[:], T.hb[:])], local_sem=S.sent)
        sent += KA
    g.remote_dma_fused([_copy(topo, direct, _spread(_common(topo, core, direct), KD), S.a1, T.ps[:], slot)],
                       local_sem=S.sent)
    sent += KD

    if raw:
        g.tensor.wait_ge(S.a3, KR)
        g.tensor.matmul(T.gq[:, 0:128], T.xn[:], T.xn[:], start=True, stop=True).then_inc(S.mm3, 1)
        g.vector.wait_ge(S.mm3, 1)
        g.vector.tensor_copy(T.gn[:], T.gq[:, 0:128]).then_inc(S.cp3, 1)

    ops = [("p", j) for j in early] + [("g", 0) for _r in raw] + [("p", j) for j in late]
    g.tensor.wait_ge(S.idn, 1)
    g.tensor.wait_ge(S.a1, KD * len(early))
    for i, (kind, j) in enumerate(ops):
        last = i == len(ops) - 1
        if kind == "g":
            g.tensor.wait_ge(S.cp3, 1)
            mm = g.tensor.matmul(T.acc[:, 0:F], T.gn[:], T.ws[:], start=False, stop=last)
        else:
            if late and j == late[0]:
                g.tensor.wait_ge(S.a2, KF * len(late))
            mm = g.tensor.matmul(T.acc[:, 0:F], T.idm[:], T.ga[:, j * F:(j + 1) * F], start=False, stop=last)
        if last:
            mm.then_inc(S.mmf, 1)
    g.vector.wait_ge(S.mmf, 1)
    g.vector.tensor_copy(T.ys[:], T.acc[:, 0:F]).then_inc(S.cpf, 1)

    g.sync.wait_ge(S.cpf, 1)
    g.sync.dma_start(T.y[:], T.ys[:]).then_inc(S.st, 16)
    g.sync.wait_ge(S.st, 16)
    g.wait_ge(S.sent, sent)
